import numpy as np
import ml_dtypes


def mxq(x, axis, fmt="e4m3"):
    dtype, down = {"e4m3": (ml_dtypes.float8_e4m3fn, 7), "e5m2": (ml_dtypes.float8_e5m2, 14)}[fmt]
    v = np.moveaxis(np.asarray(x, np.float32).astype(ml_dtypes.bfloat16).astype(np.float64), axis, -1)
    blocks = v.reshape(v.shape[:-1] + (-1, 32))
    amax = np.abs(blocks).max(-1, keepdims=True)
    byte = np.maximum(np.where(amax > 0, np.frexp(amax)[1] - 1 + 127, 0) - down, 1)
    scale = np.exp2(byte - 127.0)
    codes = (blocks / scale).astype(np.float32).astype(dtype).astype(np.float64)
    return np.moveaxis((codes * scale).reshape(v.shape), -1, axis)


WIDE = False


def mx_kscale(k):
    if not WIDE:
        return np.ones(k)
    levels = np.array([10, -10, 5, -5, 0])
    if k % 512:
        return np.exp2(np.random.permutation(np.resize(levels, k // 32))).repeat(32)
    a = np.empty((k // 512, 16))
    for p in range(k // 512):
        a[p, :8] = np.random.permutation(np.resize(levels, 8))
        for g in range(8):
            far = levels[np.abs(levels - a[p, g]) >= 10]
            a[p, g + 8] = far[np.random.randint(len(far))]
    return np.exp2(a.ravel()).repeat(32)


def f64(x):
    return np.asarray(x).astype(np.float64)


def striped(idx):
    return np.tile(idx.reshape(-1, 16).T, (8, 1)).astype(np.uint16)


def unstriped(offs):
    return offs[:16].T.reshape(-1).astype(np.int64)


def striped8(idx):
    return np.concatenate([x.reshape(-1, 16).T for x in idx]).astype(np.uint16)


def runs(offs, k):
    lists = np.stack([offs[16 * r : 16 * r + 16].T.reshape(-1) for r in range(8)]).astype(np.int64)
    return lists[np.arange(k) % 512 // 64]


def pack_weight(w):
    k, n = w.shape
    w = f64(np.asarray(w, np.float32).astype(ml_dtypes.bfloat16)).reshape(k // 32, 32, n)
    amax = np.abs(w).max(1)
    byte = np.clip(np.where(amax > 0, np.frexp(amax)[1] - 1 + 127 - 7, 1), 1, 254)
    scaled = (w * np.exp2(127.0 - byte)[:, None, :]).reshape(k, n).astype(np.float32)
    words = np.ascontiguousarray(scaled.reshape(k // 512, 128, 4, n).transpose(0, 1, 3, 2)).astype(ml_dtypes.float8_e4m3fn).view(np.uint8)
    return words, np.ascontiguousarray(byte.astype(np.uint8).reshape(k // 512, 16, n))


def unpack_weight(words, scales):
    g, p, n, _ = words.shape
    vals = np.ascontiguousarray(words).view(ml_dtypes.float8_e4m3fn).astype(np.float64) * np.repeat(np.exp2(scales.astype(np.float64) - 127.0), 8, axis=1)[..., None]
    return vals.transpose(0, 1, 3, 2).reshape(g * 512, n)

def planes(y):
    n, m = y.shape
    v = y.astype(np.float32).astype(ml_dtypes.bfloat16).astype(np.float64).reshape(n // 32, 32, m)
    top = np.abs(v).max(1)
    byte = np.clip(np.where(top > 0, np.frexp(top)[1] - 1 + 127 - 7, 1), 1, 254)
    codes = (v * np.exp2(127.0 - byte)[:, None, :]).reshape(n, m).astype(np.float32).astype(ml_dtypes.float8_e4m3fn).view(np.uint8)
    words = codes.reshape(n // 512, 128, 4, m).transpose(0, 1, 3, 2)
    return np.ascontiguousarray(words), np.ascontiguousarray(byte.astype(np.uint8).reshape(n // 512, 16, m))


K, T, S, N, H = 512, 2048, 512, 512, 512


def setup_inputs():
    n = np.random.standard_normal
    s = mx_kscale(K)[:, None]
    u = mx_kscale(S)
    packed_xT = pack_weight(n((K, T)) * s)
    packed_w1 = pack_weight(n((S, N)) / np.sqrt(S) / u[:, None])
    return {
        "x_words": packed_xT[0],
        "x_scales": packed_xT[1],
        "wa": (n((K, H)) / np.sqrt(K) / s).astype(np.float32),
        "gt": (np.random.uniform(0.5, 1.5, (S, 1)) * u[:, None]).astype(np.float32),
        "w1_words": packed_w1[0],
        "w1_scales": packed_w1[1],
        "offs": striped(np.random.permutation(T)[:S]),
        "fl": striped8(np.stack([np.random.permutation(H) for _ in range(8)])),
    }


def reference(x_words, x_scales, wa, gt, w1_words, w1_scales, offs, fl):
    xq = unpack_weight(x_words, x_scales)[:, unstriped(offs)]
    y = xq.T @ mxq(f64(wa), 0, "e4m3")
    z = f64(gt) * (y / (np.abs(y[np.arange(S)[:, None], runs(fl, S)]) + 0.5))
    out_0 = unpack_weight(w1_words, w1_scales).T @ mxq(z, 0, "e4m3")
    return (out_0,) + planes(out_0)

@@ -1,0 +1,196 @@
+from contextlib import ExitStack
+
+import concourse.mybir as mybir
+
+F32 = mybir.dt.float32
+BF16 = mybir.dt.bfloat16
+I32 = mybir.dt.int32
+U32 = mybir.dt.uint32
+U16 = mybir.dt.uint16
+U8 = mybir.dt.uint8
+FP8X4 = mybir.dt.float8_e4m3fn_x4
+ACT = mybir.ActivationFunctionType
+MULT = mybir.AluOpType.mult
+
+P = 128
+PACK = 4
+T = 2048
+S = 512
+H = 512
+HALF = 256
+CHUNK = 128
+RUN = 4
+FLOPS = 2 * 2 * 512 * 512 * 512
+
+
+def woven(ap):
+    return ap.rearrange("p (c i t) -> p c t i", i=RUN, t=PACK)
+
+
+def planes(ap):
+    return ap.rearrange("p t (c i) -> p c t i", i=RUN)
+
+
+def load_scale_rows(queue, tile, rows):
+    for q in range(4):
+        queue.dma_start(out=tile[32 * q : 32 * q + 4, :].bitcast(I32), in_=rows[4 * q : 4 * q + 4, :].bitcast(I32))
+
+
+def tile_picked_featdev_none_po_kernel(tc, x_words, x_scales, wa, gt, w1_words, w1_scales, offs, fl, out_0, out_1, out_2):
+    nc = tc.nc
+    with ExitStack() as ctx:
+        sb = ctx.enter_context(tc.tile_pool(name="sb", bufs=1))
+        ps = ctx.enter_context(tc.psum_pool(name="ps", bufs=1))
+
+        def tile(shape, dtype, name):
+            return sb.tile(shape, dtype, name=name, align_bytes=64)
+
+        offs_t = tile([P, S // 16], U16, "offs_t")
+        fl_t = tile([P, H // 16], U16, "fl_t")
+        xw = tile([P, T], U32, "xw")
+        xs = tile([P, T], U8, "xs")
+        w1w = tile([P, S], U32, "w1w")
+        w1s = tile([P, S], U8, "w1s")
+        gt_t = tile([P, PACK], F32, "gt_t")
+        wa_raw = [tile([P, PACK, HALF], F32, "wa_raw%d" % h) for h in range(2)]
+
+        warm = tile([P, 2], F32, "warm")
+        nc.vector.memset(xs[:].bitcast(I32), 0)
+        nc.vector.memset(warm[:, 0:1], 1.0)
+        nc.gpsimd.memset(w1s[:].bitcast(I32), 0)
+        wa_rows = wa.rearrange("(p t) n -> p t n", t=PACK)
+        nc.sync.dma_start(offs_t[:], offs)
+        nc.sync.dma_start(out=wa_raw[0][:], in_=wa_rows[:, :, 0:HALF])
+        nc.sync.dma_start(out=gt_t[:], in_=gt.rearrange("(p t) o -> p (t o)", t=PACK))
+        nc.sync.dma_start(fl_t[:], fl)
+        load_scale_rows(nc.sync, xs, x_scales[0])
+        nc.scalar.activation(out=warm[:, 1:2], in_=warm[:, 0:1], func=ACT.Abs_reciprocal_sqrt)
+        nc.sync.dma_start(out=xw[:].bitcast(I32), in_=x_words[0].rearrange("p n t -> p (n t)").bitcast(I32))
+        nc.sync.dma_start(out=wa_raw[1][:], in_=wa_rows[:, :, HALF:H])
+        nc.sync.dma_start(out=w1w[:].bitcast(I32), in_=w1_words[0].rearrange("p n t -> p (n t)").bitcast(I32))
+        load_scale_rows(nc.sync, w1s, w1_scales[0])
+
+        xs_picked = tile([P, S], U8, "xs_picked")
+        xs_dealt = tile([P, S], U8, "xs_dealt")
+        xw_dealt = tile([P, S], U32, "xw_dealt")
+        nc.vector.tensor_copy(out=xs_picked[:], in_=xs[:].indirect(offs_t[:]))
+        nc.vector.tensor_copy(out=xs_dealt[:].rearrange("p (t m) -> p t m", t=PACK), in_=xs_picked[:].rearrange("p (m t) -> p t m", t=PACK))
+        nc.vector.tensor_copy(out=xw_dealt[:].rearrange("p (t m) -> p m t", t=PACK), in_=xw[:].indirect(offs_t[:]))
+
+        y = [ps.tile([P, PACK, CHUNK], F32, name="y%d" % c) for c in range(4)]
+        size = tile([P, PACK, H], F32, "size")
+        root = [tile([P, H], F32, "root%d" % t) for t in range(PACK)]
+        factor = [tile([P, H], F32, "factor%d" % t) for t in range(PACK)]
+        fetched = tile([P, PACK, HALF], F32, "fetched")
+        for h in range(2):
+            wa_bf = tile([P, HALF * PACK], BF16, "wa_bf%d" % h)
+            wa_w = tile([P, HALF], U32, "wa_w%d" % h)
+            wa_s = tile([P, HALF], U8, "wa_s%d" % h)
+            if h == 0:
+                nc.scalar.copy(out=woven(wa_bf[:]), in_=planes(wa_raw[h][:]))
+            else:
+                nc.vector.tensor_copy(out=woven(wa_bf[:]), in_=planes(wa_raw[h][:]))
+            nc.vector.quantize_mx(out=wa_w[:].bitcast(FP8X4), scales=wa_s[:], in_=wa_bf[:])
+            for k in range(2):
+                c = 2 * h + k
+                cols = slice(k * CHUNK, (k + 1) * CHUNK)
+                for t in range(PACK):
+                    rows = slice(t * P, (t + 1) * P)
+                    nc.tensor.matmul_mx(out=y[c][:, t, :], lhsT=xw_dealt[:, rows].bitcast(FP8X4), lhsT_scale=xs_dealt[:, rows],
+                                        rhs=wa_w[:, cols].bitcast(FP8X4), rhs_scale=wa_s[:, cols], start=True, stop=True)
+
+        def take_size(c, ts):
+            nc.scalar.activation(out=size[:, ts, c * CHUNK : (c + 1) * CHUNK], in_=y[c][:, ts, :], func=ACT.Abs)
+
+        def make_factor(t, cols):
+            nc.scalar.activation(out=root[t][:, cols], in_=size[:, t, cols], func=ACT.Abs_reciprocal_sqrt, bias=0.5)
+            nc.vector.scalar_tensor_tensor(out=factor[t][:, cols], in0=root[t][:, cols], scalar=gt_t[:, t : t + 1],
+                                           in1=root[t][:, cols], op0=MULT, op1=MULT)
+
+        def fetch(t, first, count):
+            nc.vector.tensor_copy(out=fetched[:, t, first % HALF : first % HALF + count], in_=factor[t][:].indirect(fl_t[:, first // 16 : (first + count) // 16]))
+
+        w1w_dealt = tile([P, S], U32, "w1w_dealt")
+        w1s_dealt = tile([P, S], U8, "w1s_dealt")
+        take_size(0, slice(0, 4))
+        take_size(1, slice(0, 4))
+        make_factor(0, slice(0, HALF))
+        make_factor(1, slice(0, HALF))
+        nc.vector.tensor_copy(out=w1w_dealt[:].bitcast(I32).rearrange("p (t m) -> p t m", t=PACK), in_=w1w[:].bitcast(I32).rearrange("p (m t) -> p t m", t=PACK))
+        nc.vector.tensor_copy(out=w1s_dealt[:].rearrange("p (t m) -> p t m", t=PACK), in_=w1s[:].rearrange("p (m t) -> p t m", t=PACK))
+
+        for t in range(2):
+            take_size(2, slice(t, t + 1))
+            take_size(3, slice(t, t + 1))
+            make_factor(t, slice(HALF, H))
+
+            fetch(t, 0, HALF)
+        take_size(2, slice(2, 4))
+        take_size(3, slice(2, 4))
+        make_factor(2, slice(0, H))
+        fetch(2, 0, HALF)
+
+        nc.scalar.activation(out=root[3][:], in_=size[:, 3, :], func=ACT.Abs_reciprocal_sqrt, bias=0.5)
+        squared = tile([P, H], F32, "squared")
+        nc.scalar.activation(out=squared[:], in_=root[3][:], func=ACT.Square)
+        nc.scalar.activation(out=factor[3][:], in_=squared[:], func=ACT.Copy, scale=gt_t[:, 3:4])
+
+        out_w = tile([P, H], U32, "out_w")
+        out_s = tile([P, H], U8, "out_s")
+        out_rows = out_0.rearrange("(p t) n -> p t n", t=PACK)
+        out_words = out_1[0].rearrange("p n t -> p (n t)").bitcast(I32)
+        z_bf = [tile([P, CHUNK * PACK], BF16, "z_bf%d" % c) for c in range(4)]
+        res_bf = [tile([P, CHUNK * PACK], BF16, "res_bf%d" % c) for c in range(4)]
+
+        def scale_chunk(c):
+            nc.vector.tensor_tensor(out=woven(z_bf[c][:]), in0=planes(y[c][:]), in1=planes(fetched[:, :, c % 2 * CHUNK : (c % 2 + 1) * CHUNK]), op=MULT)
+
+        def mix_chunk(c):
+            cols = slice(c * CHUNK, (c + 1) * CHUNK)
+            z_w = tile([P, CHUNK], U32, "z_w%d" % c)
+            z_s = tile([P, CHUNK], U8, "z_s%d" % c)
+            nc.vector.quantize_mx(out=z_w[:].bitcast(FP8X4), scales=z_s[:], in_=z_bf[c][:])
+            acc = ps.tile([P, PACK, CHUNK], F32, name="acc%d" % c)
+            for t in range(PACK):
+                rows = slice(t * P, (t + 1) * P)
+                nc.tensor.matmul_mx(out=acc[:, t, :], lhsT=w1w_dealt[:, rows].bitcast(FP8X4), lhsT_scale=w1s_dealt[:, rows],
+                                    rhs=z_w[:].bitcast(FP8X4), rhs_scale=z_s[:], start=True, stop=True)
+            res = tile([P, PACK, CHUNK], F32, "res%d" % c)
+            nc.scalar.copy(out=res[:], in_=acc[:])
+            nc.sync.dma_start(out=out_rows[:, :, cols], in_=res[:])
+            if c < 3:
+                nc.scalar.copy(out=woven(res_bf[c][:]), in_=planes(acc[:]))
+            else:
+                nc.vector.tensor_copy(out=woven(res_bf[c][:]), in_=planes(res[:]))
+
+        def hand_on(c):
+            cols = slice(c * CHUNK, (c + 1) * CHUNK)
+            nc.vector.quantize_mx(out=out_w[:, cols].bitcast(FP8X4), scales=out_s[:, cols], in_=res_bf[c][:])
+            nc.sync.dma_start(out=out_words[:, cols], in_=out_w[:, cols].bitcast(I32))
+
+        fetch(3, 0, CHUNK)
+        fetch(3, CHUNK, CHUNK)
+        scale_chunk(0)
+
+        fetch(0, 2 * CHUNK, CHUNK)
+        mix_chunk(0)
+        scale_chunk(1)
+        fetch(1, 2 * CHUNK, CHUNK)
+        mix_chunk(1)
+        fetch(2, 2 * CHUNK, CHUNK)
+        fetch(3, 2 * CHUNK, CHUNK)
+        fetch(0, 3 * CHUNK, CHUNK)
+        scale_chunk(2)
+        fetch(1, 3 * CHUNK, CHUNK)
+        mix_chunk(2)
+        hand_on(0)
+        fetch(2, 3 * CHUNK, CHUNK)
+        fetch(3, 3 * CHUNK, CHUNK)
+        hand_on(1)
+        scale_chunk(3)
+        mix_chunk(3)
+        hand_on(2)
+        hand_on(3)
+        for q in range(4):
+            queue = nc.sync if q % 2 == 0 else nc.scalar
+            queue.dma_start(out=out_2[0][4 * q : 4 * q + 4, :].bitcast(I32), in_=out_s[32 * q : 32 * q + 4, :].bitcast(I32))

@@ -42,8 +42,8 @@ def tile_picked_featdev_none_po_kernel(tc, x_words, x_scales, wa, gt, w1_words, 
         sb = ctx.enter_context(tc.tile_pool(name="sb", bufs=1))
         ps = ctx.enter_context(tc.psum_pool(name="ps", bufs=1))
 
-        def tile(shape, dtype, name):
-            return sb.tile(shape, dtype, name=name, align_bytes=64)
+        def tile(shape, dtype, name, tag=None):
+            return sb.tile(shape, dtype, name=name, tag=tag or name, align_bytes=64)
 
         offs_t = tile([P, S // 16], U16, "offs_t")
         fl_t = tile([P, H // 16], U16, "fl_t")
@@ -60,12 +60,12 @@ def tile_picked_featdev_none_po_kernel(tc, x_words, x_scales, wa, gt, w1_words, 
         nc.gpsimd.memset(w1s[:].bitcast(I32), 0)
         wa_rows = wa.rearrange("(p t) n -> p t n", t=PACK)
         nc.sync.dma_start(offs_t[:], offs)
-        nc.sync.dma_start(out=wa_raw[0][:], in_=wa_rows[:, :, 0:HALF])
         nc.sync.dma_start(out=gt_t[:], in_=gt.rearrange("(p t) o -> p (t o)", t=PACK))
         nc.sync.dma_start(fl_t[:], fl)
         load_scale_rows(nc.sync, xs, x_scales[0])
         nc.scalar.activation(out=warm[:, 1:2], in_=warm[:, 0:1], func=ACT.Abs_reciprocal_sqrt)
         nc.sync.dma_start(out=xw[:].bitcast(I32), in_=x_words[0].rearrange("p n t -> p (n t)").bitcast(I32))
+        nc.sync.dma_start(out=wa_raw[0][:], in_=wa_rows[:, :, 0:HALF])
         nc.sync.dma_start(out=wa_raw[1][:], in_=wa_rows[:, :, HALF:H])
         nc.sync.dma_start(out=w1w[:].bitcast(I32), in_=w1_words[0].rearrange("p n t -> p (n t)").bitcast(I32))
         load_scale_rows(nc.sync, w1s, w1_scales[0])
@@ -78,72 +78,97 @@ def tile_picked_featdev_none_po_kernel(tc, x_words, x_scales, wa, gt, w1_words, 
         nc.vector.tensor_copy(out=xw_dealt[:].rearrange("p (t m) -> p m t", t=PACK), in_=xw[:].indirect(offs_t[:]))
 
         y = [ps.tile([P, PACK, CHUNK], F32, name="y%d" % c) for c in range(4)]
-        size = tile([P, PACK, H], F32, "size")
-        root = [tile([P, H], F32, "root%d" % t) for t in range(PACK)]
-        factor = [tile([P, H], F32, "factor%d" % t) for t in range(PACK)]
-        fetched = tile([P, PACK, HALF], F32, "fetched")
+        size = [tile([P, H], F32, "size%d" % t) for t in range(PACK)]
+        fetched = tile([P, PACK, H], F32, "fetched")
+        root = tile([P, PACK, H], F32, "root")
+        squared = tile([P, PACK, H], F32, "squared")
+        factor = tile([P, PACK, H], F32, "factor")
+        wa_w = [tile([P, HALF], U32, "wa_w%d" % h) for h in range(2)]
+        wa_s = [tile([P, HALF], U8, "wa_s%d" % h) for h in range(2)]
+        wa_bf = [tile([P, 2, CHUNK * PACK], BF16, "wa_bf%d" % h) for h in range(2)]
         for h in range(2):
-            wa_bf = tile([P, HALF * PACK], BF16, "wa_bf%d" % h)
-            wa_w = tile([P, HALF], U32, "wa_w%d" % h)
-            wa_s = tile([P, HALF], U8, "wa_s%d" % h)
-            if h == 0:
-                nc.scalar.copy(out=woven(wa_bf[:]), in_=planes(wa_raw[h][:]))
-            else:
-                nc.vector.tensor_copy(out=woven(wa_bf[:]), in_=planes(wa_raw[h][:]))
-            nc.vector.quantize_mx(out=wa_w[:].bitcast(FP8X4), scales=wa_s[:], in_=wa_bf[:])
-            for k in range(2):
-                c = 2 * h + k
-                cols = slice(k * CHUNK, (k + 1) * CHUNK)
-                for t in range(PACK):
-                    rows = slice(t * P, (t + 1) * P)
-                    nc.tensor.matmul_mx(out=y[c][:, t, :], lhsT=xw_dealt[:, rows].bitcast(FP8X4), lhsT_scale=xs_dealt[:, rows],
-                                        rhs=wa_w[:, cols].bitcast(FP8X4), rhs_scale=wa_s[:, cols], start=True, stop=True)
+            on_scalar, on_vector = h, 1 - h
+            nc.scalar.copy(out=woven(wa_bf[h][:, on_scalar, :]), in_=planes(wa_raw[h][:, :, on_scalar * CHUNK : (on_scalar + 1) * CHUNK]))
+            nc.vector.tensor_copy(out=woven(wa_bf[h][:, on_vector, :]), in_=planes(wa_raw[h][:, :, on_vector * CHUNK : (on_vector + 1) * CHUNK]))
+            nc.vector.quantize_mx(out=wa_w[h][:].bitcast(FP8X4), scales=wa_s[h][:], in_=wa_bf[h][:].rearrange("p c n -> p (c n)"))
 
-        def take_size(c, ts):
-            nc.scalar.activation(out=size[:, ts, c * CHUNK : (c + 1) * CHUNK], in_=y[c][:, ts, :], func=ACT.Abs)
+        def project(c, ts):
+            part = slice(c % 2 * CHUNK, (c % 2 + 1) * CHUNK)
+            for t in range(ts.start, ts.stop):
+                rows = slice(t * P, (t + 1) * P)
+                nc.tensor.matmul_mx(out=y[c][:, t, :], lhsT=xw_dealt[:, rows].bitcast(FP8X4), lhsT_scale=xs_dealt[:, rows],
+                                    rhs=wa_w[c // 2][:, part].bitcast(FP8X4), rhs_scale=wa_s[c // 2][:, part], start=True, stop=True)
 
-        def make_factor(t, cols):
-            nc.scalar.activation(out=root[t][:, cols], in_=size[:, t, cols], func=ACT.Abs_reciprocal_sqrt, bias=0.5)
-            nc.vector.scalar_tensor_tensor(out=factor[t][:, cols], in0=root[t][:, cols], scalar=gt_t[:, t : t + 1],
-                                           in1=root[t][:, cols], op0=MULT, op1=MULT)
+        def fetch(t, h):
+            nc.vector.tensor_copy(out=fetched[:, t, h * HALF : (h + 1) * HALF], in_=size[t][:].indirect(fl_t[:, h * 16 : (h + 1) * 16]))
 
-        def fetch(t, first, count):
-            nc.vector.tensor_copy(out=fetched[:, t, first % HALF : first % HALF + count], in_=factor[t][:].indirect(fl_t[:, first // 16 : (first + count) // 16]))
+        def take_root(ts, cols):
+            nc.scalar.activation(out=root[:, ts, cols], in_=fetched[:, ts, cols], func=ACT.Abs_reciprocal_sqrt, bias=0.5)
 
-        w1w_dealt = tile([P, S], U32, "w1w_dealt")
-        w1s_dealt = tile([P, S], U8, "w1s_dealt")
-        take_size(0, slice(0, 4))
-        take_size(1, slice(0, 4))
-        make_factor(0, slice(0, HALF))
-        make_factor(1, slice(0, HALF))
+        def square(ts, cols):
+            nc.scalar.activation(out=squared[:, ts, cols], in_=root[:, ts, cols], func=ACT.Square)
+
+        def weigh(t, cols):
+            nc.scalar.activation(out=factor[:, t, cols], in_=squared[:, t, cols], func=ACT.Copy, scale=gt_t[:, t : t + 1])
+
+        def factor_on_vector(t, cols):
+            nc.vector.scalar_tensor_tensor(out=factor[:, t, cols], in0=root[:, t, cols], scalar=gt_t[:, t : t + 1],
+                                           in1=root[:, t, cols], op0=MULT, op1=MULT)
+
+        w1w_dealt = tile([P, S], U32, "w1w_dealt", "wa_bf1")
+        w1s_dealt = tile([P, S], U8, "w1s_dealt", "wa_raw1")
         nc.vector.tensor_copy(out=w1w_dealt[:].bitcast(I32).rearrange("p (t m) -> p t m", t=PACK), in_=w1w[:].bitcast(I32).rearrange("p (m t) -> p t m", t=PACK))
         nc.vector.tensor_copy(out=w1s_dealt[:].rearrange("p (t m) -> p t m", t=PACK), in_=w1s[:].rearrange("p (m t) -> p t m", t=PACK))
 
+
+        project(0, slice(0, PACK))
+        project(1, slice(0, PACK))
+        early = []
         for t in range(2):
-            take_size(2, slice(t, t + 1))
-            take_size(3, slice(t, t + 1))
-            make_factor(t, slice(HALF, H))
-
-            fetch(t, 0, HALF)
-        take_size(2, slice(2, 4))
-        take_size(3, slice(2, 4))
-        make_factor(2, slice(0, H))
-        fetch(2, 0, HALF)
-
-        nc.scalar.activation(out=root[3][:], in_=size[:, 3, :], func=ACT.Abs_reciprocal_sqrt, bias=0.5)
-        squared = tile([P, H], F32, "squared")
-        nc.scalar.activation(out=squared[:], in_=root[3][:], func=ACT.Square)
-        nc.scalar.activation(out=factor[3][:], in_=squared[:], func=ACT.Copy, scale=gt_t[:, 3:4])
+            bank = ps.tile([P, HALF], F32, name="early%d" % t, tag="acc%d" % t)
+            rows = slice(t * P, (t + 1) * P)
+            nc.tensor.matmul_mx(out=bank[:], lhsT=xw_dealt[:, rows].bitcast(FP8X4), lhsT_scale=xs_dealt[:, rows],
+                                rhs=wa_w[1][:].bitcast(FP8X4), rhs_scale=wa_s[1][:], start=True, stop=True)
+            early.append(bank)
+        project(2, slice(0, PACK))
+        project(3, slice(0, PACK))
+        for t in range(PACK):
+            for c in range(2 if t < 2 else 4):
+                nc.scalar.activation(out=size[t][:, c * CHUNK : (c + 1) * CHUNK], in_=y[c][:, t, :], func=ACT.Abs)
+            if t < 2:
+                nc.scalar.activation(out=size[t][:, HALF:H], in_=early[t][:], func=ACT.Abs)
+            fetch(t, 0)
+            fetch(t, 1)
+        first, second = slice(0, HALF), slice(HALF, H)
+        whole = slice(0, H)
+        take_root(slice(0, 1), first)
+        take_root(slice(0, 1), second)
+        square(slice(0, 1), first)
+        square(slice(0, 1), second)
+        take_root(slice(1, 2), whole)
+        weigh(0, whole)
+        square(slice(1, 2), whole)
+        for t in range(2, 4):
+            take_root(slice(t, t + 1), first)
+            factor_on_vector(t, first)
+        weigh(1, first)
+        take_root(slice(2, 4), second)
+        weigh(1, second)
+        square(slice(2, 4), second)
+        weigh(2, second)
+        weigh(3, second)
 
         out_w = tile([P, H], U32, "out_w")
         out_s = tile([P, H], U8, "out_s")
         out_rows = out_0.rearrange("(p t) n -> p t n", t=PACK)
         out_words = out_1[0].rearrange("p n t -> p (n t)").bitcast(I32)
         z_bf = [tile([P, CHUNK * PACK], BF16, "z_bf%d" % c) for c in range(4)]
-        res_bf = [tile([P, CHUNK * PACK], BF16, "res_bf%d" % c) for c in range(4)]
+        res_bf = tile([P, 4, CHUNK * PACK], BF16, "res_bf")
+
+        res = [tile([P, PACK, CHUNK], F32, "res%d" % c) for c in range(4)]
 
         def scale_chunk(c):
-            nc.vector.tensor_tensor(out=woven(z_bf[c][:]), in0=planes(y[c][:]), in1=planes(fetched[:, :, c % 2 * CHUNK : (c % 2 + 1) * CHUNK]), op=MULT)
+            nc.vector.tensor_tensor(out=woven(z_bf[c][:]), in0=planes(y[c][:]), in1=planes(factor[:, :, c * CHUNK : (c + 1) * CHUNK]), op=MULT)
 
         def mix_chunk(c):
             cols = slice(c * CHUNK, (c + 1) * CHUNK)
@@ -155,42 +180,33 @@ def tile_picked_featdev_none_po_kernel(tc, x_words, x_scales, wa, gt, w1_words, 
                 rows = slice(t * P, (t + 1) * P)
                 nc.tensor.matmul_mx(out=acc[:, t, :], lhsT=w1w_dealt[:, rows].bitcast(FP8X4), lhsT_scale=w1s_dealt[:, rows],
                                     rhs=z_w[:].bitcast(FP8X4), rhs_scale=z_s[:], start=True, stop=True)
-            res = tile([P, PACK, CHUNK], F32, "res%d" % c)
-            nc.scalar.copy(out=res[:], in_=acc[:])
-            nc.sync.dma_start(out=out_rows[:, :, cols], in_=res[:])
-            if c < 3:
-                nc.scalar.copy(out=woven(res_bf[c][:]), in_=planes(acc[:]))
-            else:
-                nc.vector.tensor_copy(out=woven(res_bf[c][:]), in_=planes(res[:]))
+            nc.scalar.copy(out=res[c][:], in_=acc[:])
+            nc.sync.dma_start(out=out_rows[:, :, cols], in_=res[c][:])
 
-        def hand_on(c):
-            cols = slice(c * CHUNK, (c + 1) * CHUNK)
-            nc.vector.quantize_mx(out=out_w[:, cols].bitcast(FP8X4), scales=out_s[:, cols], in_=res_bf[c][:])
-            nc.sync.dma_start(out=out_words[:, cols], in_=out_w[:, cols].bitcast(I32))
+        def hand_on(first, count):
+            cols = slice(first * CHUNK, (first + count) * CHUNK)
+            nc.vector.quantize_mx(out=out_w[:, cols].bitcast(FP8X4), scales=out_s[:, cols], in_=res_bf[:, first : first + count, :].rearrange("p c n -> p (c n)"))
 
-        fetch(3, 0, CHUNK)
-        fetch(3, CHUNK, CHUNK)
+        def round_on_vector(c):
+            nc.vector.tensor_copy(out=woven(res_bf[:, c, :]), in_=planes(res[c][:]))
+
         scale_chunk(0)
-
-        fetch(0, 2 * CHUNK, CHUNK)
-        mix_chunk(0)
         scale_chunk(1)
-        fetch(1, 2 * CHUNK, CHUNK)
+        mix_chunk(0)
         mix_chunk(1)
-        fetch(2, 2 * CHUNK, CHUNK)
-        fetch(3, 2 * CHUNK, CHUNK)
-        fetch(0, 3 * CHUNK, CHUNK)
         scale_chunk(2)
-        fetch(1, 3 * CHUNK, CHUNK)
         mix_chunk(2)
-        hand_on(0)
-        fetch(2, 3 * CHUNK, CHUNK)
-        fetch(3, 3 * CHUNK, CHUNK)
-        hand_on(1)
         scale_chunk(3)
         mix_chunk(3)
-        hand_on(2)
-        hand_on(3)
+        round_on_vector(0)
+        round_on_vector(1)
+        hand_on(0, 2)
+        nc.sync.dma_start(out=out_words[:, 0:HALF], in_=out_w[:, 0:HALF].bitcast(I32))
+        round_on_vector(2)
+        round_on_vector(3)
+        hand_on(2, 1)
+        hand_on(3, 1)
+        nc.sync.dma_start(out=out_words[:, HALF:H], in_=out_w[:, HALF:H].bitcast(I32))
         for q in range(4):
             queue = nc.sync if q % 2 == 0 else nc.scalar
             queue.dma_start(out=out_2[0][4 * q : 4 * q + 4, :].bitcast(I32), in_=out_s[32 * q : 32 * q + 4, :].bitcast(I32))

@@ -40,10 +40,11 @@ def tile_picked_featdev_none_po_kernel(tc, x_words, x_scales, wa, gt, w1_words, 
     nc = tc.nc
     with ExitStack() as ctx:
         sb = ctx.enter_context(tc.tile_pool(name="sb", bufs=1))
+        reuse = ctx.enter_context(tc.tile_pool(name="reuse", bufs=1))
         ps = ctx.enter_context(tc.psum_pool(name="ps", bufs=1))
 
-        def tile(shape, dtype, name, tag=None):
-            return sb.tile(shape, dtype, name=name, tag=tag or name, align_bytes=64)
+        def tile(shape, dtype, name):
+            return sb.tile(shape, dtype, name=name, align_bytes=64)
 
         offs_t = tile([P, S // 16], U16, "offs_t")
         fl_t = tile([P, H // 16], U16, "fl_t")
@@ -52,7 +53,7 @@ def tile_picked_featdev_none_po_kernel(tc, x_words, x_scales, wa, gt, w1_words, 
         w1w = tile([P, S], U32, "w1w")
         w1s = tile([P, S], U8, "w1s")
         gt_t = tile([P, PACK], F32, "gt_t")
-        wa_raw = [tile([P, PACK, HALF], F32, "wa_raw%d" % h) for h in range(2)]
+        wa_raw = [tile([P, PACK, HALF], F32, "wa_raw0"), reuse.tile([P, PACK, HALF], F32, name="wa_raw1", align_bytes=64, offset=4 * H - 64)]
 
         warm = tile([P, 2], F32, "warm")
         nc.vector.memset(xs[:].bitcast(I32), 0)
@@ -78,14 +79,14 @@ def tile_picked_featdev_none_po_kernel(tc, x_words, x_scales, wa, gt, w1_words, 
         nc.vector.tensor_copy(out=xw_dealt[:].rearrange("p (t m) -> p m t", t=PACK), in_=xw[:].indirect(offs_t[:]))
 
         y = [ps.tile([P, PACK, CHUNK], F32, name="y%d" % c) for c in range(4)]
-        size = [tile([P, H], F32, "size%d" % t) for t in range(PACK)]
+        size = [reuse.tile([P, H], F32, name="size%d" % t, align_bytes=64, offset=4 * H * t) for t in range(PACK)]
         fetched = tile([P, PACK, H], F32, "fetched")
         root = tile([P, PACK, H], F32, "root")
         squared = tile([P, PACK, H], F32, "squared")
         factor = tile([P, PACK, H], F32, "factor")
         wa_w = [tile([P, HALF], U32, "wa_w%d" % h) for h in range(2)]
         wa_s = [tile([P, HALF], U8, "wa_s%d" % h) for h in range(2)]
-        wa_bf = [tile([P, 2, CHUNK * PACK], BF16, "wa_bf%d" % h) for h in range(2)]
+        wa_bf = [tile([P, 2, CHUNK * PACK], BF16, "wa_bf0"), reuse.tile([P, 2, CHUNK * PACK], BF16, name="wa_bf1", align_bytes=64, offset=16 * H)]
         for h in range(2):
             on_scalar, on_vector = h, 1 - h
             nc.scalar.copy(out=woven(wa_bf[h][:, on_scalar, :]), in_=planes(wa_raw[h][:, :, on_scalar * CHUNK : (on_scalar + 1) * CHUNK]))
@@ -115,8 +116,8 @@ def tile_picked_featdev_none_po_kernel(tc, x_words, x_scales, wa, gt, w1_words, 
             nc.vector.scalar_tensor_tensor(out=factor[:, t, cols], in0=root[:, t, cols], scalar=gt_t[:, t : t + 1],
                                            in1=root[:, t, cols], op0=MULT, op1=MULT)
 
-        w1w_dealt = tile([P, S], U32, "w1w_dealt", "wa_bf1")
-        w1s_dealt = tile([P, S], U8, "w1s_dealt", "wa_raw1")
+        w1w_dealt = reuse.tile([P, S], U32, name="w1w_dealt", align_bytes=64, offset=16 * H + S)
+        w1s_dealt = reuse.tile([P, S], U8, name="w1s_dealt", align_bytes=64, offset=16 * H)
         nc.vector.tensor_copy(out=w1w_dealt[:].bitcast(I32).rearrange("p (t m) -> p t m", t=PACK), in_=w1w[:].bitcast(I32).rearrange("p (m t) -> p t m", t=PACK))
         nc.vector.tensor_copy(out=w1s_dealt[:].rearrange("p (t m) -> p t m", t=PACK), in_=w1s[:].rearrange("p (m t) -> p t m", t=PACK))
 
@@ -124,7 +125,7 @@ def tile_picked_featdev_none_po_kernel(tc, x_words, x_scales, wa, gt, w1_words, 
         project(0, slice(0, PACK))
         project(1, slice(0, PACK))
         early = []
-        for t in range(2):
+        for t in range(3):
             bank = ps.tile([P, HALF], F32, name="early%d" % t, tag="acc%d" % t)
             rows = slice(t * P, (t + 1) * P)
             nc.tensor.matmul_mx(out=bank[:], lhsT=xw_dealt[:, rows].bitcast(FP8X4), lhsT_scale=xs_dealt[:, rows],
@@ -133,9 +134,9 @@ def tile_picked_featdev_none_po_kernel(tc, x_words, x_scales, wa, gt, w1_words, 
         project(2, slice(0, PACK))
         project(3, slice(0, PACK))
         for t in range(PACK):
-            for c in range(2 if t < 2 else 4):
+            for c in range(2 if t < 3 else 4):
                 nc.scalar.activation(out=size[t][:, c * CHUNK : (c + 1) * CHUNK], in_=y[c][:, t, :], func=ACT.Abs)
-            if t < 2:
+            if t < 3:
                 nc.scalar.activation(out=size[t][:, HALF:H], in_=early[t][:], func=ACT.Abs)
             fetch(t, 0)
             fetch(t, 1)

from contextlib import ExitStack

import concourse.mybir as mybir

F32 = mybir.dt.float32
BF16 = mybir.dt.bfloat16
I32 = mybir.dt.int32
U32 = mybir.dt.uint32
U16 = mybir.dt.uint16
U8 = mybir.dt.uint8
FP8X4 = mybir.dt.float8_e4m3fn_x4
ACT = mybir.ActivationFunctionType
MULT = mybir.AluOpType.mult

P = 128
PACK = 4
T = 2048
S = 512
H = 512
HALF = 256
CHUNK = 128
RUN = 4
FLOPS = 2 * 2 * 512 * 512 * 512


def woven(ap):
    return ap.rearrange("p (c i t) -> p c t i", i=RUN, t=PACK)


def planes(ap):
    return ap.rearrange("p t (c i) -> p c t i", i=RUN)


def load_scale_rows(queue, tile, rows):
    for q in range(4):
        queue.dma_start(out=tile[32 * q : 32 * q + 4, :].bitcast(I32), in_=rows[4 * q : 4 * q + 4, :].bitcast(I32))


def tile_picked_featdev_none_po_kernel(tc, x_words, x_scales, wa, gt, w1_words, w1_scales, offs, fl, out_0, out_1, out_2):
    nc = tc.nc
    with ExitStack() as ctx:
        sb = ctx.enter_context(tc.tile_pool(name="sb", bufs=1))
        reuse = ctx.enter_context(tc.tile_pool(name="reuse", bufs=1))
        ps = ctx.enter_context(tc.psum_pool(name="ps", bufs=1))

        def tile(shape, dtype, name):
            return sb.tile(shape, dtype, name=name, align_bytes=64)

        offs_t = tile([P, S // 16], U16, "offs_t")
        fl_t = tile([P, H // 16], U16, "fl_t")
        xw = tile([P, T], U32, "xw")
        xs = tile([P, T], U8, "xs")
        w1w = tile([P, S], U32, "w1w")
        w1s = tile([P, S], U8, "w1s")
        gt_t = tile([P, PACK], F32, "gt_t")
        wa_raw = [tile([P, PACK, HALF], F32, "wa_raw0"), reuse.tile([P, PACK, HALF], F32, name="wa_raw1", align_bytes=64, offset=4 * H - 64)]

        warm = tile([P, 2], F32, "warm")
        nc.vector.memset(xs[:].bitcast(I32), 0)
        nc.vector.memset(warm[:, 0:1], 1.0)
        nc.gpsimd.memset(w1s[:].bitcast(I32), 0)
        wa_rows = wa.rearrange("(p t) n -> p t n", t=PACK)
        nc.sync.dma_start(offs_t[:], offs)
        nc.sync.dma_start(out=gt_t[:], in_=gt.rearrange("(p t) o -> p (t o)", t=PACK))
        nc.sync.dma_start(fl_t[:], fl)
        load_scale_rows(nc.sync, xs, x_scales[0])
        nc.scalar.activation(out=warm[:, 1:2], in_=warm[:, 0:1], func=ACT.Abs_reciprocal_sqrt)
        nc.sync.dma_start(out=xw[:].bitcast(I32), in_=x_words[0].rearrange("p n t -> p (n t)").bitcast(I32))
        nc.sync.dma_start(out=wa_raw[0][:], in_=wa_rows[:, :, 0:HALF])
        nc.sync.dma_start(out=wa_raw[1][:], in_=wa_rows[:, :, HALF:H])
        nc.sync.dma_start(out=w1w[:].bitcast(I32), in_=w1_words[0].rearrange("p n t -> p (n t)").bitcast(I32))
        load_scale_rows(nc.sync, w1s, w1_scales[0])

        xs_picked = tile([P, S], U8, "xs_picked")
        xs_dealt = tile([P, S], U8, "xs_dealt")
        xw_dealt = tile([P, S], U32, "xw_dealt")
        nc.vector.tensor_copy(out=xs_picked[:], in_=xs[:].indirect(offs_t[:]))
        nc.vector.tensor_copy(out=xs_dealt[:].rearrange("p (t m) -> p t m", t=PACK), in_=xs_picked[:].rearrange("p (m t) -> p t m", t=PACK))
        nc.vector.tensor_copy(out=xw_dealt[:].rearrange("p (t m) -> p m t", t=PACK), in_=xw[:].indirect(offs_t[:]))

        y = [ps.tile([P, PACK, CHUNK], F32, name="y%d" % c) for c in range(4)]
        size = [reuse.tile([P, H], F32, name="size%d" % t, align_bytes=64, offset=4 * H * t) for t in range(PACK)]
        fetched = tile([P, PACK, H], F32, "fetched")
        root = tile([P, PACK, H], F32, "root")
        squared = tile([P, PACK, H], F32, "squared")
        factor = tile([P, PACK, H], F32, "factor")
        wa_w = [tile([P, HALF], U32, "wa_w%d" % h) for h in range(2)]
        wa_s = [tile([P, HALF], U8, "wa_s%d" % h) for h in range(2)]
        wa_bf = [tile([P, 2, CHUNK * PACK], BF16, "wa_bf0"), reuse.tile([P, 2, CHUNK * PACK], BF16, name="wa_bf1", align_bytes=64, offset=16 * H)]
        for h in range(2):
            on_scalar, on_vector = h, 1 - h
            nc.scalar.copy(out=woven(wa_bf[h][:, on_scalar, :]), in_=planes(wa_raw[h][:, :, on_scalar * CHUNK : (on_scalar + 1) * CHUNK]))
            nc.vector.tensor_copy(out=woven(wa_bf[h][:, on_vector, :]), in_=planes(wa_raw[h][:, :, on_vector * CHUNK : (on_vector + 1) * CHUNK]))
            nc.vector.quantize_mx(out=wa_w[h][:].bitcast(FP8X4), scales=wa_s[h][:], in_=wa_bf[h][:].rearrange("p c n -> p (c n)"))

        def project(c, ts):
            part = slice(c % 2 * CHUNK, (c % 2 + 1) * CHUNK)
            for t in range(ts.start, ts.stop):
                rows = slice(t * P, (t + 1) * P)
                nc.tensor.matmul_mx(out=y[c][:, t, :], lhsT=xw_dealt[:, rows].bitcast(FP8X4), lhsT_scale=xs_dealt[:, rows],
                                    rhs=wa_w[c // 2][:, part].bitcast(FP8X4), rhs_scale=wa_s[c // 2][:, part], start=True, stop=True)

        def fetch(t, h):
            nc.vector.tensor_copy(out=fetched[:, t, h * HALF : (h + 1) * HALF], in_=size[t][:].indirect(fl_t[:, h * 16 : (h + 1) * 16]))

        def take_root(ts, cols):
            nc.scalar.activation(out=root[:, ts, cols], in_=fetched[:, ts, cols], func=ACT.Abs_reciprocal_sqrt, bias=0.5)

        def square(ts, cols):
            nc.scalar.activation(out=squared[:, ts, cols], in_=root[:, ts, cols], func=ACT.Square)

        def weigh(t, cols):
            nc.scalar.activation(out=factor[:, t, cols], in_=squared[:, t, cols], func=ACT.Copy, scale=gt_t[:, t : t + 1])

        def factor_on_vector(t, cols):
            nc.vector.scalar_tensor_tensor(out=factor[:, t, cols], in0=root[:, t, cols], scalar=gt_t[:, t : t + 1],
                                           in1=root[:, t, cols], op0=MULT, op1=MULT)

        w1w_dealt = reuse.tile([P, S], U32, name="w1w_dealt", align_bytes=64, offset=16 * H + S)
        w1s_dealt = reuse.tile([P, S], U8, name="w1s_dealt", align_bytes=64, offset=16 * H)
        nc.vector.tensor_copy(out=w1w_dealt[:].bitcast(I32).rearrange("p (t m) -> p t m", t=PACK), in_=w1w[:].bitcast(I32).rearrange("p (m t) -> p t m", t=PACK))
        nc.vector.tensor_copy(out=w1s_dealt[:].rearrange("p (t m) -> p t m", t=PACK), in_=w1s[:].rearrange("p (m t) -> p t m", t=PACK))


        project(0, slice(0, PACK))
        project(1, slice(0, PACK))
        early = []
        for t in range(3):
            bank = ps.tile([P, HALF], F32, name="early%d" % t, tag="acc%d" % t)
            rows = slice(t * P, (t + 1) * P)
            nc.tensor.matmul_mx(out=bank[:], lhsT=xw_dealt[:, rows].bitcast(FP8X4), lhsT_scale=xs_dealt[:, rows],
                                rhs=wa_w[1][:].bitcast(FP8X4), rhs_scale=wa_s[1][:], start=True, stop=True)
            early.append(bank)
        project(2, slice(0, PACK))
        project(3, slice(0, PACK))
        for t in range(PACK):
            for c in range(2 if t < 3 else 4):
                nc.scalar.activation(out=size[t][:, c * CHUNK : (c + 1) * CHUNK], in_=y[c][:, t, :], func=ACT.Abs)
            if t < 3:
                nc.scalar.activation(out=size[t][:, HALF:H], in_=early[t][:], func=ACT.Abs)
            fetch(t, 0)
            fetch(t, 1)
        first, second = slice(0, HALF), slice(HALF, H)
        whole = slice(0, H)
        take_root(slice(0, 1), first)
        take_root(slice(0, 1), second)
        square(slice(0, 1), first)
        square(slice(0, 1), second)
        take_root(slice(1, 2), whole)
        weigh(0, whole)
        square(slice(1, 2), whole)
        for t in range(2, 4):
            take_root(slice(t, t + 1), first)
            factor_on_vector(t, first)
        weigh(1, first)
        take_root(slice(2, 4), second)
        weigh(1, second)
        square(slice(2, 4), second)
        weigh(2, second)
        weigh(3, second)

        out_w = tile([P, H], U32, "out_w")
        out_s = tile([P, H], U8, "out_s")
        out_rows = out_0.rearrange("(p t) n -> p t n", t=PACK)
        out_words = out_1[0].rearrange("p n t -> p (n t)").bitcast(I32)
        z_bf = [tile([P, CHUNK * PACK], BF16, "z_bf%d" % c) for c in range(4)]
        res_bf = tile([P, 4, CHUNK * PACK], BF16, "res_bf")

        res = [tile([P, PACK, CHUNK], F32, "res%d" % c) for c in range(4)]

        def scale_chunk(c):
            nc.vector.tensor_tensor(out=woven(z_bf[c][:]), in0=planes(y[c][:]), in1=planes(factor[:, :, c * CHUNK : (c + 1) * CHUNK]), op=MULT)

        def mix_chunk(c):
            cols = slice(c * CHUNK, (c + 1) * CHUNK)
            z_w = tile([P, CHUNK], U32, "z_w%d" % c)
            z_s = tile([P, CHUNK], U8, "z_s%d" % c)
            nc.vector.quantize_mx(out=z_w[:].bitcast(FP8X4), scales=z_s[:], in_=z_bf[c][:])
            acc = ps.tile([P, PACK, CHUNK], F32, name="acc%d" % c)
            for t in range(PACK):
                rows = slice(t * P, (t + 1) * P)
                nc.tensor.matmul_mx(out=acc[:, t, :], lhsT=w1w_dealt[:, rows].bitcast(FP8X4), lhsT_scale=w1s_dealt[:, rows],
                                    rhs=z_w[:].bitcast(FP8X4), rhs_scale=z_s[:], start=True, stop=True)
            nc.scalar.copy(out=res[c][:], in_=acc[:])
            nc.sync.dma_start(out=out_rows[:, :, cols], in_=res[c][:])

        def hand_on(first, count):
            cols = slice(first * CHUNK, (first + count) * CHUNK)
            nc.vector.quantize_mx(out=out_w[:, cols].bitcast(FP8X4), scales=out_s[:, cols], in_=res_bf[:, first : first + count, :].rearrange("p c n -> p (c n)"))

        def round_on_vector(c):
            nc.vector.tensor_copy(out=woven(res_bf[:, c, :]), in_=planes(res[c][:]))

        scale_chunk(0)
        scale_chunk(1)
        mix_chunk(0)
        mix_chunk(1)
        scale_chunk(2)
        mix_chunk(2)
        scale_chunk(3)
        mix_chunk(3)
        round_on_vector(0)
        round_on_vector(1)
        hand_on(0, 2)
        nc.sync.dma_start(out=out_words[:, 0:HALF], in_=out_w[:, 0:HALF].bitcast(I32))
        round_on_vector(2)
        round_on_vector(3)
        hand_on(2, 1)
        hand_on(3, 1)
        nc.sync.dma_start(out=out_words[:, HALF:H], in_=out_w[:, HALF:H].bitcast(I32))
        for q in range(4):
            queue = nc.sync if q % 2 == 0 else nc.scalar
            queue.dma_start(out=out_2[0][4 * q : 4 * q + 4, :].bitcast(I32), in_=out_s[32 * q : 32 * q + 4, :].bitcast(I32))
